import numpy as np
import ml_dtypes


def mxq(x, axis, fmt="e4m3"):
    dtype, down = {"e4m3": (ml_dtypes.float8_e4m3fn, 7), "e5m2": (ml_dtypes.float8_e5m2, 14)}[fmt]
    v = np.moveaxis(np.asarray(x, np.float32).astype(ml_dtypes.bfloat16).astype(np.float64), axis, -1)
    blocks = v.reshape(v.shape[:-1] + (-1, 32))
    amax = np.abs(blocks).max(-1, keepdims=True)
    byte = np.maximum(np.where(amax > 0, np.frexp(amax)[1] - 1 + 127, 0) - down, 1)
    scale = np.exp2(byte - 127.0)
    codes = (blocks / scale).astype(np.float32).astype(dtype).astype(np.float64)
    return np.moveaxis((codes * scale).reshape(v.shape), -1, axis)


WIDE = False


def mx_kscale(k):
    if not WIDE:
        return np.ones(k)
    levels = np.array([30, -30])
    if k % 512:
        return np.exp2(np.random.permutation(np.resize(levels, k // 32))).repeat(32)
    a = np.empty((k // 512, 16))
    for p in range(k // 512):
        a[p, :8] = np.random.permutation(np.resize(levels, 8))
        for g in range(8):
            far = levels[np.abs(levels - a[p, g]) >= 10]
            a[p, g + 8] = far[np.random.randint(len(far))]
    return np.exp2(a.ravel()).repeat(32)


def f64(x):
    return np.asarray(x).astype(np.float64)


def striped(idx):
    return np.tile(np.asarray(idx).reshape(-1, 16).T, (8, 1)).astype(np.uint16)


def unstriped(offs):
    return offs[:16].T.reshape(-1).astype(np.int64)


E2M1 = np.array([0.0, 0.5, 1.0, 1.5, 2.0, 3.0, 4.0, 6.0, -0.0, -0.5, -1.0, -1.5, -2.0, -3.0, -4.0, -6.0])


def pack_weight(w, fmt):
    k, n = w.shape
    w = f64(np.asarray(w, np.float32).astype(ml_dtypes.bfloat16)).reshape(k // 32, 32, n)
    amax = np.abs(w).max(1)
    if fmt in ("e4m3", "e5m2"):
        byte = np.frexp(amax)[1] - 1 + 127 - (7 if fmt == "e4m3" else 14)
    else:
        mant, ex = np.frexp(amax / 6.0)
        byte = np.where(mant > 0.5, ex, ex - 1) + 127
    byte = np.clip(np.where(amax > 0, byte, 1), 1, 254)
    scaled = (w * np.exp2(127.0 - byte)[:, None, :]).reshape(k, n).astype(np.float32)
    by_word = np.ascontiguousarray(scaled.reshape(k // 512, 128, 4, n).transpose(0, 1, 3, 2))
    if fmt in ("e4m3", "e5m2"):
        words = by_word.astype(ml_dtypes.float8_e4m3fn if fmt == "e4m3" else ml_dtypes.float8_e5m2).view(np.uint8)
    else:
        c = by_word.astype(ml_dtypes.float4_e2m1fn).view(np.uint8) & 0xF
        words = (c[..., 0::2] | (c[..., 1::2] << 4)).reshape(k // 512, 128, 2 * n)
    return np.ascontiguousarray(words), np.ascontiguousarray(byte.astype(np.uint8).reshape(k // 512, 16, n))


def unpack_weight(words, scales, fmt):
    g, _, n = scales.shape
    words = np.ascontiguousarray(words).reshape(g, 128, n, -1)
    if fmt in ("e4m3", "e5m2"):
        vals = words.view(ml_dtypes.float8_e4m3fn if fmt == "e4m3" else ml_dtypes.float8_e5m2).astype(np.float64)
    else:
        nib = np.empty((g, 128, n, 4), np.uint8)
        nib[..., 0::2] = words & 0xF
        nib[..., 1::2] = words >> 4
        vals = E2M1[nib]
    vals = vals * np.repeat(np.exp2(scales.astype(np.float64) - 127.0), 8, axis=1)[..., None]
    return vals.transpose(0, 1, 3, 2).reshape(g * 512, n)


K, T, I, J, N, Z, S, V, C = 512, 1024, 512, 256, 256, 1024, 1024, 1024, 512


def setup_inputs():
    n = np.random.standard_normal
    idx = np.random.permutation(T)[:I]
    idx2 = np.random.permutation(Z)[:J]
    idx3 = np.random.permutation(V)[:J]
    idx4 = np.random.permutation(C)[:J]
    idx5 = np.random.permutation(C)[:J]
    idx6 = np.random.permutation(S)[:N]
    fk = mx_kscale(K)
    fi = mx_kscale(I)
    ti = np.ones(T)
    ti[idx] = fi
    xkp = pack_weight(n((K, T)) * 0.3 * fk[:, None] * ti, "e2m1")
    xqp = pack_weight(n((K, Z)) * 0.3 / fk[:, None], "e4m3")
    xrp = pack_weight(n((K, V)) * 0.3 / fk[:, None], "e5m2")
    vsp = pack_weight(n((I, S)) / fi[:, None], "e4m3")
    return {
        "xk_words": xkp[0],
        "xk_scales": xkp[1],
        "xq_words": xqp[0],
        "xq_scales": xqp[1],
        "xr_words": xrp[0],
        "xr_scales": xrp[1],
        "vs_words": vsp[0],
        "vs_scales": vsp[1],
        "offs": striped(idx),
        "offs2": striped(idx2),
        "offs3": striped(idx3),
        "offs4": striped(idx4),
        "offs5": striped(idx5),
        "offs6": striped(idx6),
    }


def reference(xk_words, xk_scales, xq_words, xq_scales, xr_words, xr_scales, vs_words, vs_scales, offs, offs2, offs3, offs4, offs5, offs6):
    idx = unstriped(offs)
    idx2 = unstriped(offs2)
    idx3 = unstriped(offs3)
    idx4 = unstriped(offs4)
    idx5 = unstriped(offs5)
    idx6 = unstriped(offs6)
    xku = unpack_weight(xk_words, xk_scales, "e2m1")
    xqu = unpack_weight(xq_words, xq_scales, "e4m3")
    xru = unpack_weight(xr_words, xr_scales, "e5m2")
    vsu = unpack_weight(vs_words, vs_scales, "e4m3")
    xkidxg = xku[:, idx]
    xqidx2g = xqu[:, idx2]
    s1 = xkidxg.T @ xqidx2g
    xridx3g = xru[:, idx3]
    s2 = xkidxg.T @ xridx3g
    pw = np.zeros((I, C))
    pw[:, idx4] = s1
    hid = np.maximum(pw[:, idx5], s2)
    vsidx6g = vsu[:, idx6]
    hidq = mxq(hid, 0, "e5m2")
    y = vsidx6g.T @ hidq
    return y

@@ -1,0 +1,148 @@
+from contextlib import ExitStack
+
+import concourse.mybir as mybir
+
+K, T, I, J, N, C = 512, 1024, 512, 256, 256, 512
+FLOPS = 2 * K * I * J * 2 + 2 * I * N * J
+
+F32 = mybir.dt.float32
+BF16 = mybir.dt.bfloat16
+I32 = mybir.dt.int32
+U32 = mybir.dt.uint32
+U16 = mybir.dt.uint16
+U8 = mybir.dt.uint8
+E2M1 = mybir.dt.float4_e2m1fn_x4
+E4M3 = mybir.dt.float8_e4m3fn_x4
+E5M2 = mybir.dt.float8_e5m2_x4
+COPY = mybir.ActivationFunctionType.Copy
+MAX = mybir.AluOpType.max
+
+P = 128
+PACK = 4
+HALF = J // 2
+
+
+def tile_list_contest_rivals_board_plain_kernel(
+    tc, xk_words, xk_scales, xq_words, xq_scales, xr_words, xr_scales, vs_words, vs_scales,
+    offs, offs2, offs3, offs4, offs5, offs6, out,
+):
+    nc = tc.nc
+    with ExitStack() as ctx:
+        sb = ctx.enter_context(tc.tile_pool(name="sb", bufs=1))
+        ps = ctx.enter_context(tc.psum_pool(name="ps", bufs=1))
+
+        def load_list(name, src):
+            tile = sb.tile(list(src.shape), U16, name=name)
+            nc.sync.dma_start(tile[:], src)
+            return tile
+
+        def load_words(name, src, dtype):
+            tile = sb.tile([P, T], dtype, name=name, align_bytes=64)
+            nc.sync.dma_start(tile[:].bitcast(I32), src.bitcast(I32))
+            return tile
+
+        def load_scales(name, src, queue):
+            tile = sb.tile([P, T], U8, name=name, align_bytes=64)
+            nc.gpsimd.memset(tile[:].bitcast(I32), 0)
+            for q in range(4):
+                queue.dma_start(tile[32 * q : 32 * q + 4, :].bitcast(I32), src[0, 4 * q : 4 * q + 4, :].bitcast(I32))
+            return tile
+
+        def gather(name, window, offsets, count, dtype):
+            tile = sb.tile([P, count], dtype, name=name, align_bytes=64)
+            nc.vector.tensor_copy(tile[:], window[:].indirect(offsets[:]))
+            return tile
+
+        def flat(words):
+            return words[0].rearrange("p c r -> p (c r)")
+
+        key_list = load_list("key_list", offs)
+        xk_w = load_words("xk_w", xk_words[0], U16)
+        xk_s = load_scales("xk_s", xk_scales, nc.sync)
+        query_list = load_list("query_list", offs2)
+        xq_w = load_words("xq_w", flat(xq_words), U32)
+        xq_s = load_scales("xq_s", xq_scales, nc.sync)
+        rival_list = load_list("rival_list", offs3)
+        xr_w = load_words("xr_w", flat(xr_words), U32)
+        xr_s = load_scales("xr_s", xr_scales, nc.sync)
+        put_list = load_list("put_list", offs4)
+        read_list = load_list("read_list", offs5)
+        store_list = load_list("store_list", offs6)
+        vs_w = load_words("vs_w", flat(vs_words), U32)
+        vs_s = load_scales("vs_s", vs_scales, nc.sync)
+
+        boards = [sb.tile([P, C], F32, name="board%d" % t) for t in range(PACK)]
+        for t in range(PACK):
+            nc.vector.memset(boards[t][:], 0.0)
+
+        key_w = gather("key_w", xk_w, key_list, I, U16)
+        dealt_s = sb.tile([P, I], U8, name="dealt_s", align_bytes=64)
+        nc.vector.tensor_copy(dealt_s[:].rearrange("p (t m) -> p m t", t=PACK), xk_s[:].indirect(key_list[:]))
+        dealt_w = sb.tile([P, I], U16, name="dealt_w", align_bytes=64)
+        nc.vector.tensor_copy(
+            dealt_w[:].rearrange("p (t c i) -> p c t i", t=PACK, i=8),
+            key_w[:].rearrange("p (c i t) -> p c t i", t=PACK, i=8),
+        )
+        query_w = gather("query_w", xq_w, query_list, J, U32)
+        query_s = gather("query_s", xq_s, query_list, J, U8)
+
+        def scores(acc, t, words, scales, fmt, cols):
+            rows = slice(t * P, (t + 1) * P)
+            nc.tensor.matmul_mx(
+                out=acc, lhsT=dealt_w[:, rows].bitcast(E2M1), lhsT_scale=dealt_s[:, rows],
+                rhs=words[:, cols].bitcast(fmt), rhs_scale=scales[:, cols], start=True, stop=True,
+            )
+
+        s1_banks = [ps.tile([P, 2, J], F32, name="s1_bank%d" % b) for b in range(2)]
+        for t in range(PACK):
+            scores(s1_banks[t // 2][:, t % 2, :], t, query_w, query_s, E4M3, slice(0, J))
+
+        rival_w = gather("rival_w", xr_w, rival_list, J, U32)
+        rival_s = gather("rival_s", xr_s, rival_list, J, U8)
+        s2_banks = [ps.tile([P, PACK, HALF], F32, name="s2_bank%d" % h) for h in range(2)]
+        for h in range(2):
+            for t in range(PACK):
+                scores(s2_banks[h][:, t, :], t, rival_w, rival_s, E5M2, slice(h * HALF, (h + 1) * HALF))
+
+        store_w = gather("store_w", vs_w, store_list, N, U32)
+        store_s = gather("store_s", vs_s, store_list, N, U8)
+
+        s1 = [sb.tile([P, 2, J], F32, name="s1_%d" % b) for b in range(2)]
+        for b in range(2):
+            nc.scalar.copy(s1[b][:], s1_banks[b][:])
+            nc.scalar.activation(boards[2 * b][:].indirect(put_list[:]), s1[b][:, 0, :], COPY)
+            nc.vector.tensor_copy(boards[2 * b + 1][:].indirect(put_list[:]), s1[b][:, 1, :])
+
+        picked = sb.tile([P, PACK, J], F32, name="picked")
+        for t in (0, 2, 1):
+            nc.scalar.activation(picked[:, t, :], boards[t][:].indirect(read_list[:]), COPY)
+        nc.vector.tensor_copy(picked[:, 3, :], boards[3][:].indirect(read_list[:]))
+
+        hid = [sb.tile([P, HALF * PACK], BF16, name="hid%d" % h, align_bytes=64) for h in range(2)]
+        for h in range(2):
+            nc.vector.tensor_tensor(
+                hid[h][:].rearrange("p (c i t) -> p c t i", t=PACK, i=4),
+                picked[:, :, h * HALF : (h + 1) * HALF].rearrange("p t (c i) -> p c t i", i=4),
+                s2_banks[h][:].rearrange("p t (c i) -> p c t i", i=4),
+                MAX,
+            )
+        hid_w = [sb.tile([P, HALF], U32, name="hid_w%d" % h, align_bytes=64) for h in range(2)]
+        hid_s = [sb.tile([P, HALF], U8, name="hid_s%d" % h, align_bytes=64) for h in range(2)]
+        for h in range(2):
+            nc.vector.quantize_mx(out=hid_w[h][:].bitcast(E5M2), scales=hid_s[h][:], in_=hid[h][:])
+
+        out_rows = out.rearrange("(b p) j -> p b j", p=P)
+        for h in range(2):
+            bank = ps.tile([P, 2, HALF], F32, name="out_bank%d" % h)
+            for b in range(2):
+                cols = slice(b * P, (b + 1) * P)
+                nc.tensor.matmul_mx(
+                    out=bank[:, b, :], lhsT=store_w[:, cols].bitcast(E4M3), lhsT_scale=store_s[:, cols],
+                    rhs=hid_w[h][:].bitcast(E5M2), rhs_scale=hid_s[h][:], start=True, stop=True,
+                )
+            result = sb.tile([P, 2, HALF], F32, name="result%d" % h)
+            if h == 0:
+                nc.scalar.copy(result[:], bank[:])
+            else:
+                nc.vector.tensor_copy(result[:], bank[:])
+            nc.sync.dma_start(out_rows[:, :, h * HALF : (h + 1) * HALF], result[:])

@@ -42,7 +42,7 @@ def tile_list_contest_rivals_board_plain_kernel(
             return tile
 
         def load_scales(name, src, queue):
-            tile = sb.tile([P, T], U8, name=name, align_bytes=64)
+            tile = sb.tile([P, T], U8, name=name, tag=name, align_bytes=64)
             nc.gpsimd.memset(tile[:].bitcast(I32), 0)
             for q in range(4):
                 queue.dma_start(tile[32 * q : 32 * q + 4, :].bitcast(I32), src[0, 4 * q : 4 * q + 4, :].bitcast(I32))
@@ -56,8 +56,8 @@ def tile_list_contest_rivals_board_plain_kernel(
         def flat(words):
             return words[0].rearrange("p c r -> p (c r)")
 
-        key_list = load_list("key_list", offs)
         xk_w = load_words("xk_w", xk_words[0], U16)
+        key_list = load_list("key_list", offs)
         xk_s = load_scales("xk_s", xk_scales, nc.sync)
         query_list = load_list("query_list", offs2)
         xq_w = load_words("xq_w", flat(xq_words), U32)
@@ -65,11 +65,11 @@ def tile_list_contest_rivals_board_plain_kernel(
         rival_list = load_list("rival_list", offs3)
         xr_w = load_words("xr_w", flat(xr_words), U32)
         xr_s = load_scales("xr_s", xr_scales, nc.sync)
-        put_list = load_list("put_list", offs4)
-        read_list = load_list("read_list", offs5)
         store_list = load_list("store_list", offs6)
         vs_w = load_words("vs_w", flat(vs_words), U32)
+        put_list = load_list("put_list", offs4)
         vs_s = load_scales("vs_s", vs_scales, nc.sync)
+        read_list = load_list("read_list", offs5)
 
         boards = [sb.tile([P, C], F32, name="board%d" % t) for t in range(PACK)]
         for t in range(PACK):
@@ -78,24 +78,27 @@ def tile_list_contest_rivals_board_plain_kernel(
         key_w = gather("key_w", xk_w, key_list, I, U16)
         dealt_s = sb.tile([P, I], U8, name="dealt_s", align_bytes=64)
         nc.vector.tensor_copy(dealt_s[:].rearrange("p (t m) -> p m t", t=PACK), xk_s[:].indirect(key_list[:]))
-        dealt_w = sb.tile([P, I], U16, name="dealt_w", align_bytes=64)
-        nc.vector.tensor_copy(
-            dealt_w[:].rearrange("p (t c i) -> p c t i", t=PACK, i=8),
-            key_w[:].rearrange("p (c i t) -> p c t i", t=PACK, i=8),
-        )
+        key_slices = key_w[:].rearrange("p (c i t) -> p c t i", t=PACK, i=8)
+        first_w = sb.tile([P, P], U16, name="first_w", align_bytes=64)
+        nc.vector.tensor_copy(first_w[:].rearrange("p (c i) -> p c i", i=8), key_slices[:, :, 0, :])
         query_w = gather("query_w", xq_w, query_list, J, U32)
         query_s = gather("query_s", xq_s, query_list, J, U8)
+        other_w = sb.tile([P, (PACK - 1) * P], U16, name="other_w", tag="xq_s", align_bytes=64)
+        nc.vector.tensor_copy(other_w[:].rearrange("p (t c i) -> p c t i", t=PACK - 1, i=8), key_slices[:, :, 1:PACK, :])
+        dealt_w = [first_w[:]] + [other_w[:, t * P : (t + 1) * P] for t in range(PACK - 1)]
 
         def scores(acc, t, words, scales, fmt, cols):
             rows = slice(t * P, (t + 1) * P)
             nc.tensor.matmul_mx(
-                out=acc, lhsT=dealt_w[:, rows].bitcast(E2M1), lhsT_scale=dealt_s[:, rows],
+                out=acc, lhsT=dealt_w[t].bitcast(E2M1), lhsT_scale=dealt_s[:, rows],
                 rhs=words[:, cols].bitcast(fmt), rhs_scale=scales[:, cols], start=True, stop=True,
             )
 
-        s1_banks = [ps.tile([P, 2, J], F32, name="s1_bank%d" % b) for b in range(2)]
-        for t in range(PACK):
-            scores(s1_banks[t // 2][:, t % 2, :], t, query_w, query_s, E4M3, slice(0, J))
+        s1_bank0 = ps.tile([P, J], F32, name="s1_bank0")
+        s1_bank13 = ps.tile([P, 2, J], F32, name="s1_bank13")
+        s1_bank2 = ps.tile([P, J], F32, name="s1_bank2")
+        for t, acc in ((0, s1_bank0[:]), (1, s1_bank13[:, 0, :]), (3, s1_bank13[:, 1, :]), (2, s1_bank2[:])):
+            scores(acc, t, query_w, query_s, E4M3, slice(0, J))
 
         rival_w = gather("rival_w", xr_w, rival_list, J, U32)
         rival_s = gather("rival_s", xr_s, rival_list, J, U8)
@@ -107,42 +110,57 @@ def tile_list_contest_rivals_board_plain_kernel(
         store_w = gather("store_w", vs_w, store_list, N, U32)
         store_s = gather("store_s", vs_s, store_list, N, U8)
 
-        s1 = [sb.tile([P, 2, J], F32, name="s1_%d" % b) for b in range(2)]
-        for b in range(2):
-            nc.scalar.copy(s1[b][:], s1_banks[b][:])
-            nc.scalar.activation(boards[2 * b][:].indirect(put_list[:]), s1[b][:, 0, :], COPY)
-            nc.vector.tensor_copy(boards[2 * b + 1][:].indirect(put_list[:]), s1[b][:, 1, :])
+        s1_0 = sb.tile([P, J], F32, name="s1_0")
+        nc.scalar.copy(s1_0[:], s1_bank0[:])
+        s1_13 = sb.tile([P, 2, J], F32, name="s1_13")
+        nc.scalar.copy(s1_13[:], s1_bank13[:])
+        nc.scalar.activation(boards[0][:].indirect(put_list[:]), s1_0[:], COPY)
+        s1_2 = sb.tile([P, J], F32, name="s1_2")
+        nc.scalar.copy(s1_2[:], s1_bank2[:])
+        nc.scalar.activation(boards[2][:].indirect(put_list[:]), s1_2[:], COPY)
+        nc.vector.tensor_copy(boards[1][:].indirect(put_list[:]), s1_13[:, 0, :])
+        nc.vector.tensor_copy(boards[3][:].indirect(put_list[:]), s1_13[:, 1, :])
 
         picked = sb.tile([P, PACK, J], F32, name="picked")
-        for t in (0, 2, 1):
+        for t in (0, 2):
             nc.scalar.activation(picked[:, t, :], boards[t][:].indirect(read_list[:]), COPY)
-        nc.vector.tensor_copy(picked[:, 3, :], boards[3][:].indirect(read_list[:]))
+        for t in (1, 3):
+            nc.vector.tensor_copy(picked[:, t, 0:HALF], boards[t][:].indirect(read_list[:, 0 : HALF // 16]))
+        for t in (1, 3):
+            nc.scalar.activation(picked[:, t, HALF:J], boards[t][:].indirect(read_list[:, HALF // 16 : J // 16]), COPY)
 
-        hid = [sb.tile([P, HALF * PACK], BF16, name="hid%d" % h, align_bytes=64) for h in range(2)]
+        out_rows = out.rearrange("(b p) j -> p b j", p=P)
         for h in range(2):
+            hid = sb.tile([P, HALF * PACK], BF16, name="hid%d" % h, tag=("vs_s", "xr_s")[h], align_bytes=64)
             nc.vector.tensor_tensor(
-                hid[h][:].rearrange("p (c i t) -> p c t i", t=PACK, i=4),
+                hid[:].rearrange("p (c i t) -> p c t i", t=PACK, i=4),
                 picked[:, :, h * HALF : (h + 1) * HALF].rearrange("p t (c i) -> p c t i", i=4),
                 s2_banks[h][:].rearrange("p t (c i) -> p c t i", i=4),
                 MAX,
             )
-        hid_w = [sb.tile([P, HALF], U32, name="hid_w%d" % h, align_bytes=64) for h in range(2)]
-        hid_s = [sb.tile([P, HALF], U8, name="hid_s%d" % h, align_bytes=64) for h in range(2)]
-        for h in range(2):
-            nc.vector.quantize_mx(out=hid_w[h][:].bitcast(E5M2), scales=hid_s[h][:], in_=hid[h][:])
+            hid_w = sb.tile([P, HALF], U32, name="hid_w%d" % h, align_bytes=64)
+            hid_s = sb.tile([P, HALF], U8, name="hid_s%d" % h, align_bytes=64)
+            nc.vector.quantize_mx(out=hid_w[:].bitcast(E5M2), scales=hid_s[:], in_=hid[:])
 
-        out_rows = out.rearrange("(b p) j -> p b j", p=P)
-        for h in range(2):
-            bank = ps.tile([P, 2, HALF], F32, name="out_bank%d" % h)
+            if h == 0:
+                bank = ps.tile([P, 2, HALF], F32, name="out_bank")
+                accs = [bank[:, 0, :], bank[:, 1, :]]
+            else:
+                accs = [ps.tile([P, HALF], F32, name="out_last%d" % b)[:] for b in range(2)]
             for b in range(2):
                 cols = slice(b * P, (b + 1) * P)
                 nc.tensor.matmul_mx(
-                    out=bank[:, b, :], lhsT=store_w[:, cols].bitcast(E4M3), lhsT_scale=store_s[:, cols],
-                    rhs=hid_w[h][:].bitcast(E5M2), rhs_scale=hid_s[h][:], start=True, stop=True,
+                    out=accs[b], lhsT=store_w[:, cols].bitcast(E4M3), lhsT_scale=store_s[:, cols],
+                    rhs=hid_w[:].bitcast(E5M2), rhs_scale=hid_s[:], start=True, stop=True,
                 )
-            result = sb.tile([P, 2, HALF], F32, name="result%d" % h)
             if h == 0:
+                result = sb.tile([P, 2, HALF], F32, name="result")
                 nc.scalar.copy(result[:], bank[:])
+                nc.sync.dma_start(out_rows[:, :, 0:HALF], result[:])
             else:
-                nc.vector.tensor_copy(result[:], bank[:])
-            nc.sync.dma_start(out_rows[:, :, h * HALF : (h + 1) * HALF], result[:])
+                last0 = sb.tile([P, HALF], F32, name="last0")
+                nc.vector.tensor_copy(last0[:], accs[0])
+                nc.sync.dma_start(out_rows[:, 0, HALF:J], last0[:])
+                last1 = sb.tile([P, HALF], F32, name="last1")
+                nc.scalar.copy(last1[:], accs[1])
+                nc.scalar.dma_start(out_rows[:, 1, HALF:J], last1[:])

@@ -48,8 +48,8 @@ def tile_list_contest_rivals_board_plain_kernel(
                 queue.dma_start(tile[32 * q : 32 * q + 4, :].bitcast(I32), src[0, 4 * q : 4 * q + 4, :].bitcast(I32))
             return tile
 
-        def gather(name, window, offsets, count, dtype):
-            tile = sb.tile([P, count], dtype, name=name, align_bytes=64)
+        def gather(name, window, offsets, count, dtype, tag=None):
+            tile = sb.tile([P, count], dtype, name=name, tag=tag or name, align_bytes=64)
             nc.vector.tensor_copy(tile[:], window[:].indirect(offsets[:]))
             return tile
 
@@ -79,13 +79,13 @@ def tile_list_contest_rivals_board_plain_kernel(
         dealt_s = sb.tile([P, I], U8, name="dealt_s", align_bytes=64)
         nc.vector.tensor_copy(dealt_s[:].rearrange("p (t m) -> p m t", t=PACK), xk_s[:].indirect(key_list[:]))
         key_slices = key_w[:].rearrange("p (c i t) -> p c t i", t=PACK, i=8)
-        first_w = sb.tile([P, P], U16, name="first_w", align_bytes=64)
-        nc.vector.tensor_copy(first_w[:].rearrange("p (c i) -> p c i", i=8), key_slices[:, :, 0, :])
+        first_w = sb.tile([P, 2 * P], U16, name="first_w", align_bytes=64)
+        nc.vector.tensor_copy(first_w[:].rearrange("p (t c i) -> p c t i", t=2, i=8), key_slices[:, :, 0:2, :])
         query_w = gather("query_w", xq_w, query_list, J, U32)
         query_s = gather("query_s", xq_s, query_list, J, U8)
-        other_w = sb.tile([P, (PACK - 1) * P], U16, name="other_w", tag="xq_s", align_bytes=64)
-        nc.vector.tensor_copy(other_w[:].rearrange("p (t c i) -> p c t i", t=PACK - 1, i=8), key_slices[:, :, 1:PACK, :])
-        dealt_w = [first_w[:]] + [other_w[:, t * P : (t + 1) * P] for t in range(PACK - 1)]
+        other_w = sb.tile([P, 2 * P], U16, name="other_w", tag="xq_s", align_bytes=64)
+        nc.vector.tensor_copy(other_w[:].rearrange("p (t c i) -> p c t i", t=2, i=8), key_slices[:, :, 2:4, :])
+        dealt_w = [pair[:, u * P : (u + 1) * P] for pair in (first_w, other_w) for u in range(2)]
 
         def scores(acc, t, words, scales, fmt, cols):
             rows = slice(t * P, (t + 1) * P)
@@ -94,38 +94,35 @@ def tile_list_contest_rivals_board_plain_kernel(
                 rhs=words[:, cols].bitcast(fmt), rhs_scale=scales[:, cols], start=True, stop=True,
             )
 
-        s1_bank0 = ps.tile([P, J], F32, name="s1_bank0")
-        s1_bank13 = ps.tile([P, 2, J], F32, name="s1_bank13")
-        s1_bank2 = ps.tile([P, J], F32, name="s1_bank2")
-        for t, acc in ((0, s1_bank0[:]), (1, s1_bank13[:, 0, :]), (3, s1_bank13[:, 1, :]), (2, s1_bank2[:])):
-            scores(acc, t, query_w, query_s, E4M3, slice(0, J))
+        s1_banks = [ps.tile([P, J], F32, name="s1_bank%d" % t, tag="s1_bank%d" % t) for t in range(PACK)]
+        for t in (1, 0, 2, 3):
+            scores(s1_banks[t][:], t, query_w, query_s, E4M3, slice(0, J))
 
         rival_w = gather("rival_w", xr_w, rival_list, J, U32)
-        rival_s = gather("rival_s", xr_s, rival_list, J, U8)
+
+        s1 = [sb.tile([P, J], F32, name="s1_%d" % t, tag="s1_%d" % t, align_bytes=64) for t in range(PACK)]
+        nc.scalar.copy(s1[1][:], s1_banks[1][:])
+        nc.scalar.copy(s1[0][:], s1_banks[0][:])
+        nc.vector.tensor_copy(boards[1][:].indirect(put_list[:]), s1[1][:])
+        nc.scalar.activation(boards[0][:].indirect(put_list[:]), s1[0][:], COPY)
+        rival_s = gather("rival_s", xr_s, rival_list, J, U8, tag="s1_1")
+        store_w = gather("store_w", vs_w, store_list, N, U32)
+        nc.scalar.copy(s1[2][:], s1_banks[2][:])
+        nc.scalar.copy(s1[3][:], s1_banks[3][:])
+        nc.scalar.activation(boards[2][:].indirect(put_list[:]), s1[2][:], COPY)
+        nc.vector.tensor_copy(boards[3][:].indirect(put_list[:]), s1[3][:])
         s2_banks = [ps.tile([P, PACK, HALF], F32, name="s2_bank%d" % h) for h in range(2)]
         for h in range(2):
             for t in range(PACK):
                 scores(s2_banks[h][:, t, :], t, rival_w, rival_s, E5M2, slice(h * HALF, (h + 1) * HALF))
 
-        store_w = gather("store_w", vs_w, store_list, N, U32)
-        store_s = gather("store_s", vs_s, store_list, N, U8)
-
-        s1_0 = sb.tile([P, J], F32, name="s1_0")
-        nc.scalar.copy(s1_0[:], s1_bank0[:])
-        s1_13 = sb.tile([P, 2, J], F32, name="s1_13")
-        nc.scalar.copy(s1_13[:], s1_bank13[:])
-        nc.scalar.activation(boards[0][:].indirect(put_list[:]), s1_0[:], COPY)
-        s1_2 = sb.tile([P, J], F32, name="s1_2")
-        nc.scalar.copy(s1_2[:], s1_bank2[:])
-        nc.scalar.activation(boards[2][:].indirect(put_list[:]), s1_2[:], COPY)
-        nc.vector.tensor_copy(boards[1][:].indirect(put_list[:]), s1_13[:, 0, :])
-        nc.vector.tensor_copy(boards[3][:].indirect(put_list[:]), s1_13[:, 1, :])
 
         picked = sb.tile([P, PACK, J], F32, name="picked")
         for t in (0, 2):
             nc.scalar.activation(picked[:, t, :], boards[t][:].indirect(read_list[:]), COPY)
         for t in (1, 3):
             nc.vector.tensor_copy(picked[:, t, 0:HALF], boards[t][:].indirect(read_list[:, 0 : HALF // 16]))
+        store_s = gather("store_s", vs_s, store_list, N, U8, tag="s1_3")
         for t in (1, 3):
             nc.scalar.activation(picked[:, t, HALF:J], boards[t][:].indirect(read_list[:, HALF // 16 : J // 16]), COPY)
 
@@ -143,10 +140,10 @@ def tile_list_contest_rivals_board_plain_kernel(
             nc.vector.quantize_mx(out=hid_w[:].bitcast(E5M2), scales=hid_s[:], in_=hid[:])
 
             if h == 0:
-                bank = ps.tile([P, 2, HALF], F32, name="out_bank")
+                bank = ps.tile([P, 2, HALF], F32, name="out_bank", tag="s1_bank0")
                 accs = [bank[:, 0, :], bank[:, 1, :]]
             else:
-                accs = [ps.tile([P, HALF], F32, name="out_last%d" % b)[:] for b in range(2)]
+                accs = [ps.tile([P, HALF], F32, name="out_last%d" % b, tag="s1_bank%d" % (b + 1))[:] for b in range(2)]
             for b in range(2):
                 cols = slice(b * P, (b + 1) * P)
                 nc.tensor.matmul_mx(

from contextlib import ExitStack

import concourse.mybir as mybir

K, T, I, J, N, C = 512, 1024, 512, 256, 256, 512
FLOPS = 2 * K * I * J * 2 + 2 * I * N * J

F32 = mybir.dt.float32
BF16 = mybir.dt.bfloat16
I32 = mybir.dt.int32
U32 = mybir.dt.uint32
U16 = mybir.dt.uint16
U8 = mybir.dt.uint8
E2M1 = mybir.dt.float4_e2m1fn_x4
E4M3 = mybir.dt.float8_e4m3fn_x4
E5M2 = mybir.dt.float8_e5m2_x4
COPY = mybir.ActivationFunctionType.Copy
MAX = mybir.AluOpType.max

P = 128
PACK = 4
HALF = J // 2


def tile_list_contest_rivals_board_plain_kernel(
    tc, xk_words, xk_scales, xq_words, xq_scales, xr_words, xr_scales, vs_words, vs_scales,
    offs, offs2, offs3, offs4, offs5, offs6, out,
):
    nc = tc.nc
    with ExitStack() as ctx:
        sb = ctx.enter_context(tc.tile_pool(name="sb", bufs=1))
        ps = ctx.enter_context(tc.psum_pool(name="ps", bufs=1))

        def load_list(name, src):
            tile = sb.tile(list(src.shape), U16, name=name)
            nc.sync.dma_start(tile[:], src)
            return tile

        def load_words(name, src, dtype):
            tile = sb.tile([P, T], dtype, name=name, align_bytes=64)
            nc.sync.dma_start(tile[:].bitcast(I32), src.bitcast(I32))
            return tile

        def load_scales(name, src, queue):
            tile = sb.tile([P, T], U8, name=name, tag=name, align_bytes=64)
            nc.gpsimd.memset(tile[:].bitcast(I32), 0)
            for q in range(4):
                queue.dma_start(tile[32 * q : 32 * q + 4, :].bitcast(I32), src[0, 4 * q : 4 * q + 4, :].bitcast(I32))
            return tile

        def gather(name, window, offsets, count, dtype, tag=None):
            tile = sb.tile([P, count], dtype, name=name, tag=tag or name, align_bytes=64)
            nc.vector.tensor_copy(tile[:], window[:].indirect(offsets[:]))
            return tile

        def flat(words):
            return words[0].rearrange("p c r -> p (c r)")

        xk_w = load_words("xk_w", xk_words[0], U16)
        key_list = load_list("key_list", offs)
        xk_s = load_scales("xk_s", xk_scales, nc.sync)
        query_list = load_list("query_list", offs2)
        xq_w = load_words("xq_w", flat(xq_words), U32)
        xq_s = load_scales("xq_s", xq_scales, nc.sync)
        rival_list = load_list("rival_list", offs3)
        xr_w = load_words("xr_w", flat(xr_words), U32)
        xr_s = load_scales("xr_s", xr_scales, nc.sync)
        store_list = load_list("store_list", offs6)
        vs_w = load_words("vs_w", flat(vs_words), U32)
        put_list = load_list("put_list", offs4)
        vs_s = load_scales("vs_s", vs_scales, nc.sync)
        read_list = load_list("read_list", offs5)

        boards = [sb.tile([P, C], F32, name="board%d" % t) for t in range(PACK)]
        for t in range(PACK):
            nc.vector.memset(boards[t][:], 0.0)

        key_w = gather("key_w", xk_w, key_list, I, U16)
        dealt_s = sb.tile([P, I], U8, name="dealt_s", align_bytes=64)
        nc.vector.tensor_copy(dealt_s[:].rearrange("p (t m) -> p m t", t=PACK), xk_s[:].indirect(key_list[:]))
        key_slices = key_w[:].rearrange("p (c i t) -> p c t i", t=PACK, i=8)
        first_w = sb.tile([P, 2 * P], U16, name="first_w", align_bytes=64)
        nc.vector.tensor_copy(first_w[:].rearrange("p (t c i) -> p c t i", t=2, i=8), key_slices[:, :, 0:2, :])
        query_w = gather("query_w", xq_w, query_list, J, U32)
        query_s = gather("query_s", xq_s, query_list, J, U8)
        other_w = sb.tile([P, 2 * P], U16, name="other_w", tag="xq_s", align_bytes=64)
        nc.vector.tensor_copy(other_w[:].rearrange("p (t c i) -> p c t i", t=2, i=8), key_slices[:, :, 2:4, :])
        dealt_w = [pair[:, u * P : (u + 1) * P] for pair in (first_w, other_w) for u in range(2)]

        def scores(acc, t, words, scales, fmt, cols):
            rows = slice(t * P, (t + 1) * P)
            nc.tensor.matmul_mx(
                out=acc, lhsT=dealt_w[t].bitcast(E2M1), lhsT_scale=dealt_s[:, rows],
                rhs=words[:, cols].bitcast(fmt), rhs_scale=scales[:, cols], start=True, stop=True,
            )

        s1_banks = [ps.tile([P, J], F32, name="s1_bank%d" % t, tag="s1_bank%d" % t) for t in range(PACK)]
        for t in (1, 0, 2, 3):
            scores(s1_banks[t][:], t, query_w, query_s, E4M3, slice(0, J))

        rival_w = gather("rival_w", xr_w, rival_list, J, U32)

        s1 = [sb.tile([P, J], F32, name="s1_%d" % t, tag="s1_%d" % t, align_bytes=64) for t in range(PACK)]
        nc.scalar.copy(s1[1][:], s1_banks[1][:])
        nc.scalar.copy(s1[0][:], s1_banks[0][:])
        nc.vector.tensor_copy(boards[1][:].indirect(put_list[:]), s1[1][:])
        nc.scalar.activation(boards[0][:].indirect(put_list[:]), s1[0][:], COPY)
        rival_s = gather("rival_s", xr_s, rival_list, J, U8, tag="s1_1")
        store_w = gather("store_w", vs_w, store_list, N, U32)
        nc.scalar.copy(s1[2][:], s1_banks[2][:])
        nc.scalar.copy(s1[3][:], s1_banks[3][:])
        nc.scalar.activation(boards[2][:].indirect(put_list[:]), s1[2][:], COPY)
        nc.vector.tensor_copy(boards[3][:].indirect(put_list[:]), s1[3][:])
        s2_banks = [ps.tile([P, PACK, HALF], F32, name="s2_bank%d" % h) for h in range(2)]
        for h in range(2):
            for t in range(PACK):
                scores(s2_banks[h][:, t, :], t, rival_w, rival_s, E5M2, slice(h * HALF, (h + 1) * HALF))


        picked = sb.tile([P, PACK, J], F32, name="picked")
        for t in (0, 2):
            nc.scalar.activation(picked[:, t, :], boards[t][:].indirect(read_list[:]), COPY)
        for t in (1, 3):
            nc.vector.tensor_copy(picked[:, t, 0:HALF], boards[t][:].indirect(read_list[:, 0 : HALF // 16]))
        store_s = gather("store_s", vs_s, store_list, N, U8, tag="s1_3")
        for t in (1, 3):
            nc.scalar.activation(picked[:, t, HALF:J], boards[t][:].indirect(read_list[:, HALF // 16 : J // 16]), COPY)

        out_rows = out.rearrange("(b p) j -> p b j", p=P)
        for h in range(2):
            hid = sb.tile([P, HALF * PACK], BF16, name="hid%d" % h, tag=("vs_s", "xr_s")[h], align_bytes=64)
            nc.vector.tensor_tensor(
                hid[:].rearrange("p (c i t) -> p c t i", t=PACK, i=4),
                picked[:, :, h * HALF : (h + 1) * HALF].rearrange("p t (c i) -> p c t i", i=4),
                s2_banks[h][:].rearrange("p t (c i) -> p c t i", i=4),
                MAX,
            )
            hid_w = sb.tile([P, HALF], U32, name="hid_w%d" % h, align_bytes=64)
            hid_s = sb.tile([P, HALF], U8, name="hid_s%d" % h, align_bytes=64)
            nc.vector.quantize_mx(out=hid_w[:].bitcast(E5M2), scales=hid_s[:], in_=hid[:])

            if h == 0:
                bank = ps.tile([P, 2, HALF], F32, name="out_bank", tag="s1_bank0")
                accs = [bank[:, 0, :], bank[:, 1, :]]
            else:
                accs = [ps.tile([P, HALF], F32, name="out_last%d" % b, tag="s1_bank%d" % (b + 1))[:] for b in range(2)]
            for b in range(2):
                cols = slice(b * P, (b + 1) * P)
                nc.tensor.matmul_mx(
                    out=accs[b], lhsT=store_w[:, cols].bitcast(E4M3), lhsT_scale=store_s[:, cols],
                    rhs=hid_w[:].bitcast(E5M2), rhs_scale=hid_s[:], start=True, stop=True,
                )
            if h == 0:
                result = sb.tile([P, 2, HALF], F32, name="result")
                nc.scalar.copy(result[:], bank[:])
                nc.sync.dma_start(out_rows[:, :, 0:HALF], result[:])
            else:
                last0 = sb.tile([P, HALF], F32, name="last0")
                nc.vector.tensor_copy(last0[:], accs[0])
                nc.sync.dma_start(out_rows[:, 0, HALF:J], last0[:])
                last1 = sb.tile([P, HALF], F32, name="last1")
                nc.scalar.copy(last1[:], accs[1])
                nc.scalar.dma_start(out_rows[:, 1, HALF:J], last1[:])
